import numpy as np
import ml_dtypes


def mxq(x, axis, fmt="e4m3"):
    dtype, down = {"e4m3": (ml_dtypes.float8_e4m3fn, 7), "e5m2": (ml_dtypes.float8_e5m2, 14)}[fmt]
    v = np.moveaxis(np.asarray(x, np.float32).astype(ml_dtypes.bfloat16).astype(np.float64), axis, -1)
    blocks = v.reshape(v.shape[:-1] + (-1, 32))
    amax = np.abs(blocks).max(-1, keepdims=True)
    byte = np.maximum(np.where(amax > 0, np.frexp(amax)[1] - 1 + 127, 0) - down, 1)
    scale = np.exp2(byte - 127.0)
    codes = (blocks / scale).astype(np.float32).astype(dtype).astype(np.float64)
    return np.moveaxis((codes * scale).reshape(v.shape), -1, axis)


WIDE = False


def mx_kscale(k):
    if not WIDE:
        return np.ones(k)
    levels = np.array([10, -10, 5, -5, 0])
    if k % 512:
        return np.exp2(np.random.permutation(np.resize(levels, k // 32))).repeat(32)
    a = np.empty((k // 512, 16))
    for p in range(k // 512):
        a[p, :8] = np.random.permutation(np.resize(levels, 8))
        for g in range(8):
            far = levels[np.abs(levels - a[p, g]) >= 10]
            a[p, g + 8] = far[np.random.randint(len(far))]
    return np.exp2(a.ravel()).repeat(32)


def f64(x):
    return np.asarray(x).astype(np.float64)


def striped(idx):
    return np.tile(idx.reshape(-1, 16).T, (8, 1)).astype(np.uint16)


def unstriped(offs):
    return offs[:16].T.reshape(-1).astype(np.int64)


E2M1 = np.array([0.0, 0.5, 1.0, 1.5, 2.0, 3.0, 4.0, 6.0, -0.0, -0.5, -1.0, -1.5, -2.0, -3.0, -4.0, -6.0])


def pack_weight(w, fmt):
    k, n = w.shape
    w = f64(np.asarray(w, np.float32).astype(ml_dtypes.bfloat16)).reshape(k // 32, 32, n)
    amax = np.abs(w).max(1)
    if fmt == "e4m3":
        byte = np.frexp(amax)[1] - 1 + 127 - 7
    else:
        mant, ex = np.frexp(amax / 6.0)
        byte = np.where(mant > 0.5, ex, ex - 1) + 127
    byte = np.clip(np.where(amax > 0, byte, 1), 1, 254)
    scaled = (w * np.exp2(127.0 - byte)[:, None, :]).reshape(k, n).astype(np.float32)
    by_word = np.ascontiguousarray(scaled.reshape(k // 512, 128, 4, n).transpose(0, 1, 3, 2))
    if fmt == "e4m3":
        words = by_word.astype(ml_dtypes.float8_e4m3fn).view(np.uint8)
    else:
        c = by_word.astype(ml_dtypes.float4_e2m1fn).view(np.uint8) & 0xF
        words = (c[..., 0::2] | (c[..., 1::2] << 4)).reshape(k // 512, 128, 2 * n)
    return np.ascontiguousarray(words), np.ascontiguousarray(byte.astype(np.uint8).reshape(k // 512, 16, n))


def unpack_weight(words, scales, fmt):
    g, _, n = scales.shape
    words = np.ascontiguousarray(words).reshape(g, 128, n, -1)
    if fmt == "e4m3":
        vals = words.view(ml_dtypes.float8_e4m3fn).astype(np.float64)
    else:
        nib = np.empty((g, 128, n, 4), np.uint8)
        nib[..., 0::2] = words & 0xF
        nib[..., 1::2] = words >> 4
        vals = E2M1[nib]
    vals = vals * np.repeat(np.exp2(scales.astype(np.float64) - 127.0), 8, axis=1)[..., None]
    return vals.transpose(0, 1, 3, 2).reshape(g * 512, n)


def gelu(v):
    return 0.5 * v * (1.0 + np.tanh(np.sqrt(2.0 / np.pi) * (v + 0.044715 * v**3)))


K, KL, KM, H, T, S, P = 1536, 1024, 512, 1024, 4096, 1024, 512

def setup_inputs():
    n = np.random.standard_normal
    s = mx_kscale(K)[:, None]
    u = mx_kscale(H)
    tab_words, tab_scales = pack_weight(n((K, T)) * s, "e4m3")
    w4_words, w4_scales = pack_weight(0.55 * n((KL, H)) / np.sqrt(K) / s[:KL], "e2m1")
    return {
        "tab_words": tab_words, "tab_scales": tab_scales,
        "offs": striped(np.random.permutation(T)[:S]),
        "pos1": striped(np.random.permutation(S)[:P]),
        "pos2": striped(np.random.permutation(S)[:P]),
        "w4_words": w4_words, "w4_scales": w4_scales,
        "w1": (0.55 * n((KM, H)) / np.sqrt(K) / s[KL:]).astype(np.float32),
        "gain": (np.exp(0.3 * n(H)) * u).astype(np.float32),
        "latin": (2.5 * n(H) / np.sqrt(H) / u ** 2).astype(np.float32),
        "row": np.exp(0.3 * n(P)).astype(np.float32),
        "order": (0.5 * n((P, P))).astype(np.float32),
    }

def reference(tab_words, tab_scales, offs, pos1, pos2, w4_words, w4_scales, w1, gain, latin, row, order):
    v = unpack_weight(tab_words, tab_scales, "e4m3")[:, unstriped(offs)]
    w4 = unpack_weight(w4_words, w4_scales, "e2m1")
    w1q = mxq(f64(w1), 0, "e4m3")
    g = w4.T @ v[:KL] + w1q.T @ v[KL:]
    h = f64(gain)[:, None] * np.maximum(g, np.sin(g))
    x1 = f64(latin)[:, None] * h[:, unstriped(pos1)]
    x2 = np.abs(h[:, unstriped(pos2)])
    e = mxq(x1, 0, "e4m3").T @ mxq(x2, 0, "e4m3")
    return e * f64(row)[None, :] + f64(order)

@@ -1,0 +1,299 @@
+import math
+from contextlib import ExitStack
+
+import concourse.mybir as mybir
+from concourse.masks import make_identity
+
+K, KL, KM, H, T, S, NP = 1536, 1024, 512, 1024, 4096, 1024, 512
+FLOPS = 2 * K * H * S + 2 * H * NP * NP
+
+F32 = mybir.dt.float32
+BF16 = mybir.dt.bfloat16
+I32 = mybir.dt.int32
+U32 = mybir.dt.uint32
+U16 = mybir.dt.uint16
+U8 = mybir.dt.uint8
+FP8X4 = mybir.dt.float8_e4m3fn_x4
+FP4X4 = mybir.dt.float4_e2m1fn_x4
+ALU = mybir.AluOpType
+ACT = mybir.ActivationFunctionType
+
+P = 128
+BANK = 512
+TWO_PI = 2.0 * math.pi
+
+
+def tile_list_bilingual_verse_correspondence_kernel(
+    tc, tab_words, tab_scales, offs, pos1, pos2, w4_words, w4_scales, w1, gain, latin, row, order, out
+):
+    nc = tc.nc
+    with ExitStack() as ctx:
+        keep = ctx.enter_context(tc.tile_pool(name="keep", bufs=1))
+        work = ctx.enter_context(tc.tile_pool(name="work", bufs=2))
+        psum = ctx.enter_context(tc.psum_pool(name="psum", bufs=8))
+
+        offs_sb = keep.tile([P, S // 16], U16, name="offs_sb")
+        pos1_sb = keep.tile([P, NP // 16], U16, name="pos1_sb")
+        pos2_sb = keep.tile([P, NP // 16], U16, name="pos2_sb")
+        table = [keep.tile([P, T], I32, name="table%d" % a, align_bytes=64) for a in range(3)]
+        table_scales = keep.tile([P, T], U8, name="table_scales", align_bytes=64)
+        v_codes = [keep.tile([P, S], U32, name="v_codes%d" % a, align_bytes=64) for a in range(3)]
+        v_scales = keep.tile([P, S], U8, name="v_scales", align_bytes=64)
+        v_scales1 = keep.tile([P, S], U8, name="v_scales1", align_bytes=64)
+        w4_raw = keep.tile([P, 2 * 2 * H], U8, name="w4_raw", align_bytes=64)
+        w4_codes = keep.tile([P, 2 * 2 * H], U8, name="w4_codes", align_bytes=64)
+        w4s_raw = keep.tile([P, 2 * H], U8, name="w4s_raw", align_bytes=64)
+        w4s = keep.tile([P, 2 * H], U8, name="w4s", align_bytes=64)
+        factors_raw = keep.tile([P, 2 * P], F32, name="factors_raw")
+        ident = keep.tile([P, P], F32, name="ident")
+        factors = keep.tile([P, 2, 8], F32, name="factors")
+        both = keep.tile([P, 2, 4], F32, name="both")
+        row_sb = keep.tile([P, NP], F32, name="row_sb")
+        order_sb = keep.tile([P, 4, NP], F32, name="order_sb")
+
+        nc.vector.memset(table_scales[:].bitcast(I32), 0)
+        nc.vector.memset(w4s_raw[:].bitcast(I32), 0)
+        nc.vector.memset(v_scales1[:].bitcast(I32), 0)
+        nc.gpsimd.memset(factors_raw[:], 0.0)
+        for first, vec in ((0, gain), (4, latin)):
+            nc.gpsimd.dma_start(
+                out=factors_raw[first : first + 4, :].rearrange("t (bq i) -> t bq i", i=8),
+                in_=vec.rearrange("(bq t i) -> t bq i", t=4, i=8),
+            )
+        make_identity(nc, ident[:])
+
+        def load_table(a):
+            nc.sync.dma_start(out=table[a][:], in_=tab_words[a].rearrange("p t i -> p (t i)").bitcast(I32))
+
+        w1_rows = w1.rearrange("(p j) c -> p j c", j=4)
+        w1_raw = {}
+
+        def load_w1(b):
+            w1_raw[b] = work.tile([P, 4, BANK], F32, name="w1_raw")
+            nc.sync.dma_start(out=w1_raw[b][:], in_=w1_rows[:, :, BANK * b : BANK * (b + 1)])
+
+        nc.sync.dma_start(offs_sb[:], offs)
+        load_table(0)
+        for q in range(4):
+            nc.scalar.dma_start(
+                out=table_scales[32 * q : 32 * q + 12, :].bitcast(I32),
+                in_=tab_scales[:, 4 * q : 4 * q + 4, :].bitcast(I32),
+            )
+        nc.sync.dma_start(
+            out=w4_raw[:].bitcast(I32).rearrange("p (a c) -> p a c", a=2),
+            in_=w4_words.bitcast(I32).rearrange("a p c -> p a c"),
+        )
+        load_w1(0)
+        for q in range(4):
+            nc.scalar.dma_start(
+                out=w4s_raw[32 * q : 32 * q + 4, :].bitcast(I32).rearrange("r (a c) -> r a c", a=2),
+                in_=w4_scales[:, 4 * q : 4 * q + 4, :].bitcast(I32).rearrange("a r c -> r a c"),
+            )
+        load_table(1)
+        load_table(2)
+        nc.sync.dma_start(pos2_sb[:], pos2)
+        nc.sync.dma_start(pos1_sb[:], pos1)
+        load_w1(1)
+        nc.sync.dma_start(out=order_sb[:], in_=order.rearrange("(mt p) j -> p mt j", p=P))
+        nc.sync.dma_start(out=row_sb[:], in_=row.partition_broadcast(P))
+
+        turned = psum.tile([P, BANK], F32, name="bank")
+        for b in range(2):
+            nc.tensor.transpose(turned[:, P * b : P * (b + 1)], factors_raw[:, P * b : P * (b + 1)], ident[:])
+        nc.vector.tensor_copy(out=factors[:], in_=turned[:, 0 : 2 * P].rearrange("p (b c) -> p b c", b=2)[:, :, 0:8])
+        nc.vector.tensor_tensor(both[:], factors[:, :, 0:4], factors[:, :, 4:8], ALU.mult)
+
+        def gather_table(a, half):
+            cols = slice(BANK * half, BANK * (half + 1))
+            nc.vector.tensor_copy(
+                v_codes[a][:, cols], table[a][:].bitcast(U32).indirect(offs_sb[:, 32 * half : 32 * (half + 1)])
+            )
+
+        w1_codes, w1_scales, w1_bf = {}, {}, {}
+
+        def round_w1(i):
+            b, t = divmod(i, 4)
+            w1_bf[i] = work.tile([P, BANK], BF16, name="w1_bf", align_bytes=64)
+            nc.scalar.copy(
+                out=w1_bf[i][:].rearrange("p (q h l j) -> p q h j l", h=2, l=4, j=4),
+                in_=w1_raw[b][:].rearrange("p j (q t h l) -> p t q h j l", t=4, h=2, l=4)[:, t],
+            )
+
+        def quantize_w1(i):
+            w1_codes[i] = work.tile([P, P], U32, name="w1_codes", bufs=8, align_bytes=64)
+            w1_scales[i] = work.tile([P, P], U8, name="w1_scales", bufs=8, align_bytes=64)
+            nc.vector.quantize_mx(out=w1_codes[i][:].bitcast(FP8X4), scales=w1_scales[i][:], in_=w1_bf[i][:])
+
+        gather_table(0, 0)
+        gather_table(0, 1)
+        nc.vector.tensor_copy(v_scales[:], table_scales[:].indirect(offs_sb[:]))
+        nc.sync.dma_start(out=v_scales1[0:112, :].bitcast(I32), in_=v_scales[4:116, :].bitcast(I32))
+        for raw, dealt, w in ((w4_raw, w4_codes, 4), (w4s_raw, w4s, 2)):
+            nc.vector.tensor_copy(
+                out=dealt[:].bitcast(I32).rearrange("p (g t q w) -> p g t q w", t=4, q=16, w=w),
+                in_=raw[:].bitcast(I32).rearrange("p (g q t w) -> p g t q w", t=4, q=16, w=w),
+            )
+        for i in range(4):
+            round_w1(i)
+            quantize_w1(i)
+        gather_table(1, 0)
+        gather_table(1, 1)
+        gather_table(2, 0)
+        gather_table(2, 1)
+
+        banks = {}
+
+        def stage1_pass(i, half, a):
+            cols = slice(BANK * half, BANK * (half + 1))
+            if a == 0:
+                banks[i, half] = psum.tile([P, BANK], F32, name="bank")
+            if a < 2:
+                c0 = H * a + P * i
+                lhsT = w4_codes[:, 2 * c0 : 2 * (c0 + P)].bitcast(FP4X4)
+                lhsT_scale = w4s[:, c0 : c0 + P]
+                rhs_scale = (v_scales, v_scales1)[a][:, cols]
+            else:
+                lhsT = w1_codes[i][:].bitcast(FP8X4)
+                lhsT_scale = w1_scales[i][:]
+                rhs_scale = v_scales[8:P, cols]
+            nc.tensor.matmul_mx(
+                out=banks[i, half][:],
+                lhsT=lhsT,
+                lhsT_scale=lhsT_scale,
+                rhs=v_codes[a][:, cols].bitcast(FP8X4),
+                rhs_scale=rhs_scale,
+                start=(a == 0),
+                stop=(a == 2),
+            )
+
+        wraps, angle, sine, read, picked, planes, x_codes, x_scales = {}, {}, {}, {}, {}, {}, {}, {}
+
+        def count_turns(i):
+            turns = work.tile([P, S], U32, name="turns")
+            wraps[i] = work.tile([P, S], F32, name="wraps")
+            for half in range(2):
+                cols = slice(BANK * half, BANK * (half + 1))
+                nc.scalar.activation(turns[:, cols], banks[i, half][:], ACT.Relu, bias=0.0, scale=-1.0 / TWO_PI)
+                nc.scalar.activation(wraps[i][:, cols], turns[:, cols], ACT.Copy, scale=TWO_PI)
+
+        def reduce_angle(i):
+            angle[i] = work.tile([P, S], F32, name="angle", bufs=3)
+            for half in range(2):
+                cols = slice(BANK * half, BANK * (half + 1))
+                nc.vector.scalar_tensor_tensor(
+                    angle[i][:, cols], banks[i, half][:], 0.0, wraps[i][:, cols], ALU.min, ALU.add
+                )
+
+        def take_sine(i):
+            sine[i] = work.tile([P, S], F32, name="sine")
+            for half in range(2):
+                cols = slice(BANK * half, BANK * (half + 1))
+                nc.scalar.activation(sine[i][:, cols], angle[i][:, cols], ACT.Sin)
+
+        def take_max(i):
+            read[i] = work.tile([P, S], F32, name="read", bufs=3)
+            for half in range(2):
+                cols = slice(BANK * half, BANK * (half + 1))
+                nc.vector.tensor_tensor(read[i][:, cols], banks[i, half][:], sine[i][:, cols], ALU.max)
+
+        def pick(i):
+            for side, pos in ((2, pos2_sb), (1, pos1_sb)):
+                picked[side, i] = work.tile([P, NP], F32, name="picked", bufs=4)
+                nc.vector.tensor_copy(picked[side, i][:], read[i][:].indirect(pos[:]))
+
+        def scale_and_round(i):
+            b, t = divmod(i, 4)
+            for side, func, factor in (
+                (2, ACT.Abs, factors[:, b, t : t + 1]),
+                (1, ACT.Copy, both[:, b, t : t + 1]),
+            ):
+                if t == 0:
+                    planes[side, b] = work.tile([P, 4, NP], BF16, name="planes", bufs=4)
+                nc.scalar.activation(planes[side, b][:, t, :], picked[side, i][:], func, scale=factor)
+
+        def weave(copy, side, b, cols):
+            copy(
+                out=woven[side, b][:, cols, :].rearrange("p (c l) t -> p c t l", l=4),
+                in_=planes[side, b][:, :, cols].rearrange("p t (c l) -> p c t l", l=4),
+            )
+
+        def quantize_x(side, b, cols):
+            nc.vector.quantize_mx(
+                out=x_codes[side, b][:, cols].bitcast(FP8X4),
+                scales=x_scales[side, b][:, cols],
+                in_=woven[side, b][:, cols, :].rearrange("p c t -> p (c t)"),
+            )
+
+        def stage2_pass(mt, b):
+            cols = slice(P * mt, P * (mt + 1))
+            if b == 0:
+                e_banks[mt] = psum.tile([P, BANK], F32, name="bank")
+            nc.tensor.matmul_mx(
+                out=e_banks[mt][:],
+                lhsT=x_codes[1, b][:, cols].bitcast(FP8X4),
+                lhsT_scale=x_scales[1, b][:, cols],
+                rhs=x_codes[2, b][:].bitcast(FP8X4),
+                rhs_scale=x_scales[2, b][:],
+                start=(b == 0),
+                stop=(b == 1),
+            )
+
+        woven, e_banks = {}, {}
+        for b in range(2):
+            for side in (2, 1):
+                woven[side, b] = keep.tile([P, NP, 4], BF16, name="woven%d%d" % (side, b), align_bytes=64)
+                x_codes[side, b] = keep.tile([P, NP], U32, name="x_codes%d%d" % (side, b), align_bytes=64)
+                x_scales[side, b] = keep.tile([P, NP], U8, name="x_scales%d%d" % (side, b), align_bytes=64)
+        whole = slice(0, NP)
+
+        for a in range(2):
+            for half in range(2):
+                for i in range(4):
+                    stage1_pass(i, half, a)
+        for i in range(4):
+            for half in range(2):
+                stage1_pass(i, half, 2)
+
+        for i in range(2):
+            count_turns(i)
+            reduce_angle(i)
+        for step in range(8):
+            if 4 <= step + 3 < 8:
+                for half in range(2):
+                    for a in range(3):
+                        stage1_pass(step + 3, half, a)
+            take_sine(step)
+            take_max(step)
+            pick(step)
+            if step + 2 < 8:
+                count_turns(step + 2)
+                reduce_angle(step + 2)
+            if step < 4:
+                round_w1(step + 4)
+                quantize_w1(step + 4)
+            if step > 0:
+                scale_and_round(step - 1)
+            if step in (5, 6):
+                side = 7 - step
+                weave(nc.scalar.copy, side, 0, whole)
+                quantize_x(side, 0, whole)
+        for mt in range(4):
+            stage2_pass(mt, 0)
+        scale_and_round(7)
+        weave(nc.vector.tensor_copy, 2, 1, whole)
+        for mt in range(4):
+            weave(nc.scalar.copy, 1, 1, slice(P * mt, P * (mt + 1)))
+        quantize_x(2, 1, whole)
+        for mt in range(4):
+            quantize_x(1, 1, slice(P * mt, P * (mt + 1)))
+            stage2_pass(mt, 1)
+        scaled = {}
+        for step in range(5):
+            if step < 4:
+                scaled[step] = work.tile([P, NP], F32, name="scaled")
+                nc.vector.tensor_tensor(scaled[step][:], e_banks[step][:], row_sb[:], ALU.mult)
+            if step > 0:
+                mt = step - 1
+                result = work.tile([P, NP], F32, name="result", bufs=4)
+                nc.vector.tensor_tensor(result[:], scaled[mt][:], order_sb[:, mt, :], ALU.add)
+                nc.sync.dma_start(out=out[P * mt : P * (mt + 1), :], in_=result[:])

@@ -35,7 +35,8 @@ def tile_list_bilingual_verse_correspondence_kernel(
         offs_sb = keep.tile([P, S // 16], U16, name="offs_sb")
         pos1_sb = keep.tile([P, NP // 16], U16, name="pos1_sb")
         pos2_sb = keep.tile([P, NP // 16], U16, name="pos2_sb")
-        table = [keep.tile([P, T], I32, name="table%d" % a, align_bytes=64) for a in range(3)]
+        table = [keep.tile([P, T], I32, name="table%d" % a, tag="table%d" % a, align_bytes=64) for a in range(3)]
+        scales_raw = keep.tile([P, T], U8, name="scales_raw", align_bytes=64)
         table_scales = keep.tile([P, T], U8, name="table_scales", align_bytes=64)
         v_codes = [keep.tile([P, S], U32, name="v_codes%d" % a, align_bytes=64) for a in range(3)]
         v_scales = keep.tile([P, S], U8, name="v_scales", align_bytes=64)
@@ -52,7 +53,7 @@ def tile_list_bilingual_verse_correspondence_kernel(
         order_sb = keep.tile([P, 4, NP], F32, name="order_sb")
 
         nc.vector.memset(table_scales[:].bitcast(I32), 0)
-        nc.vector.memset(w4s_raw[:].bitcast(I32), 0)
+        nc.vector.memset(w4s[:].bitcast(I32), 0)
         nc.vector.memset(v_scales1[:].bitcast(I32), 0)
         nc.gpsimd.memset(factors_raw[:], 0.0)
         for first, vec in ((0, gain), (4, latin)):
@@ -68,40 +69,39 @@ def tile_list_bilingual_verse_correspondence_kernel(
         w1_rows = w1.rearrange("(p j) c -> p j c", j=4)
         w1_raw = {}
 
-        def load_w1(b):
-            w1_raw[b] = work.tile([P, 4, BANK], F32, name="w1_raw")
+        def load_w1(b, tag):
+            w1_raw[b] = keep.tile([P, 4, BANK], F32, name="w1_raw%d" % b, tag=tag, align_bytes=64)
             nc.sync.dma_start(out=w1_raw[b][:], in_=w1_rows[:, :, BANK * b : BANK * (b + 1)])
 
         nc.sync.dma_start(offs_sb[:], offs)
         load_table(0)
         for q in range(4):
-            nc.scalar.dma_start(
-                out=table_scales[32 * q : 32 * q + 12, :].bitcast(I32),
+            nc.sync.dma_start(
+                out=scales_raw[32 * q : 32 * q + 12, :].bitcast(I32),
                 in_=tab_scales[:, 4 * q : 4 * q + 4, :].bitcast(I32),
             )
         nc.sync.dma_start(
             out=w4_raw[:].bitcast(I32).rearrange("p (a c) -> p a c", a=2),
             in_=w4_words.bitcast(I32).rearrange("a p c -> p a c"),
         )
-        load_w1(0)
+        load_w1(0, "w1_first")
         for q in range(4):
-            nc.scalar.dma_start(
+            nc.sync.dma_start(
                 out=w4s_raw[32 * q : 32 * q + 4, :].bitcast(I32).rearrange("r (a c) -> r a c", a=2),
                 in_=w4_scales[:, 4 * q : 4 * q + 4, :].bitcast(I32).rearrange("a r c -> r a c"),
             )
-        load_table(1)
         load_table(2)
+        load_table(1)
         nc.sync.dma_start(pos2_sb[:], pos2)
         nc.sync.dma_start(pos1_sb[:], pos1)
-        load_w1(1)
         nc.sync.dma_start(out=order_sb[:], in_=order.rearrange("(mt p) j -> p mt j", p=P))
         nc.sync.dma_start(out=row_sb[:], in_=row.partition_broadcast(P))
 
         turned = psum.tile([P, BANK], F32, name="bank")
         for b in range(2):
             nc.tensor.transpose(turned[:, P * b : P * (b + 1)], factors_raw[:, P * b : P * (b + 1)], ident[:])
-        nc.vector.tensor_copy(out=factors[:], in_=turned[:, 0 : 2 * P].rearrange("p (b c) -> p b c", b=2)[:, :, 0:8])
-        nc.vector.tensor_tensor(both[:], factors[:, :, 0:4], factors[:, :, 4:8], ALU.mult)
+        nc.scalar.copy(out=factors[:], in_=turned[:, 0 : 2 * P].rearrange("p (b c) -> p b c", b=2)[:, :, 0:8])
+        nc.gpsimd.tensor_tensor(both[:], factors[:, :, 0:4], factors[:, :, 4:8], ALU.mult)
 
         def gather_table(a, half):
             cols = slice(BANK * half, BANK * (half + 1))
@@ -124,22 +124,31 @@ def tile_list_bilingual_verse_correspondence_kernel(
             w1_scales[i] = work.tile([P, P], U8, name="w1_scales", bufs=8, align_bytes=64)
             nc.vector.quantize_mx(out=w1_codes[i][:].bitcast(FP8X4), scales=w1_scales[i][:], in_=w1_bf[i][:])
 
-        gather_table(0, 0)
-        gather_table(0, 1)
+        for q in range(4):
+            rows = slice(32 * q, 32 * q + 12)
+            nc.vector.tensor_copy(table_scales[rows, :].bitcast(I32), scales_raw[rows, :].bitcast(I32))
         nc.vector.tensor_copy(v_scales[:], table_scales[:].indirect(offs_sb[:]))
-        nc.sync.dma_start(out=v_scales1[0:112, :].bitcast(I32), in_=v_scales[4:116, :].bitcast(I32))
-        for raw, dealt, w in ((w4_raw, w4_codes, 4), (w4s_raw, w4s, 2)):
+        nc.scalar.dma_start(out=v_scales1[0:112, :].bitcast(I32), in_=v_scales[4:116, :].bitcast(I32))
+        for half in range(2):
+            gather_table(0, half)
+
+        def deal(dealt, raw, w):
             nc.vector.tensor_copy(
-                out=dealt[:].bitcast(I32).rearrange("p (g t q w) -> p g t q w", t=4, q=16, w=w),
-                in_=raw[:].bitcast(I32).rearrange("p (g q t w) -> p g t q w", t=4, q=16, w=w),
+                out=dealt.bitcast(I32).rearrange("p (g t q w) -> p g t q w", t=4, q=16, w=w),
+                in_=raw.bitcast(I32).rearrange("p (g q t w) -> p g t q w", t=4, q=16, w=w),
             )
+
+        deal(w4_codes[:], w4_raw[:], 4)
+        for q in range(4):
+            deal(w4s[32 * q : 32 * q + 4, :], w4s_raw[32 * q : 32 * q + 4, :], 2)
         for i in range(4):
             round_w1(i)
             quantize_w1(i)
-        gather_table(1, 0)
-        gather_table(1, 1)
-        gather_table(2, 0)
-        gather_table(2, 1)
+        for a in (2, 1):
+            for half in range(2):
+                gather_table(a, half)
+
+        load_w1(1, "table1")
 
         banks = {}
 
@@ -163,25 +172,25 @@ def tile_list_bilingual_verse_correspondence_kernel(
                 rhs=v_codes[a][:, cols].bitcast(FP8X4),
                 rhs_scale=rhs_scale,
                 start=(a == 0),
-                stop=(a == 2),
+                stop=(a == 1),
             )
 
-        wraps, angle, sine, read, picked, planes, x_codes, x_scales = {}, {}, {}, {}, {}, {}, {}, {}
+        turns, angle, sine, read, picked, planes, x_codes, x_scales = {}, {}, {}, {}, {}, {}, {}, {}
 
         def count_turns(i):
-            turns = work.tile([P, S], U32, name="turns")
-            wraps[i] = work.tile([P, S], F32, name="wraps")
+            g_sb = work.tile([P, S], F32, name="g_sb")
+            turns[i] = work.tile([P, S], I32, name="turns")
             for half in range(2):
                 cols = slice(BANK * half, BANK * (half + 1))
-                nc.scalar.activation(turns[:, cols], banks[i, half][:], ACT.Relu, bias=0.0, scale=-1.0 / TWO_PI)
-                nc.scalar.activation(wraps[i][:, cols], turns[:, cols], ACT.Copy, scale=TWO_PI)
+                nc.scalar.copy(g_sb[:, cols], banks[i, half][:])
+                nc.gpsimd.tensor_scalar(turns[i][:, cols], g_sb[:, cols], 1.0 / TWO_PI, 0.0, ALU.mult, ALU.add)
 
         def reduce_angle(i):
             angle[i] = work.tile([P, S], F32, name="angle", bufs=3)
             for half in range(2):
                 cols = slice(BANK * half, BANK * (half + 1))
                 nc.vector.scalar_tensor_tensor(
-                    angle[i][:, cols], banks[i, half][:], 0.0, wraps[i][:, cols], ALU.min, ALU.add
+                    angle[i][:, cols], turns[i][:, cols], -TWO_PI, banks[i, half][:], ALU.mult, ALU.add
                 )
 
         def take_sine(i):
@@ -246,28 +255,27 @@ def tile_list_bilingual_verse_correspondence_kernel(
                 x_scales[side, b] = keep.tile([P, NP], U8, name="x_scales%d%d" % (side, b), align_bytes=64)
         whole = slice(0, NP)
 
-        for a in range(2):
+        for a in (0, 2):
             for half in range(2):
                 for i in range(4):
                     stage1_pass(i, half, a)
         for i in range(4):
             for half in range(2):
-                stage1_pass(i, half, 2)
+                stage1_pass(i, half, 1)
 
-        for i in range(2):
-            count_turns(i)
-            reduce_angle(i)
+        count_turns(0)
+        reduce_angle(0)
         for step in range(8):
             if 4 <= step + 3 < 8:
                 for half in range(2):
-                    for a in range(3):
+                    for a in (0, 2, 1):
                         stage1_pass(step + 3, half, a)
             take_sine(step)
             take_max(step)
             pick(step)
-            if step + 2 < 8:
-                count_turns(step + 2)
-                reduce_angle(step + 2)
+            for ahead in range(max(1, step + 2 if step else 1), min(step + 3, 8)):
+                count_turns(ahead)
+                reduce_angle(ahead)
             if step < 4:
                 round_w1(step + 4)
                 quantize_w1(step + 4)
@@ -290,10 +298,10 @@ def tile_list_bilingual_verse_correspondence_kernel(
         scaled = {}
         for step in range(5):
             if step < 4:
-                scaled[step] = work.tile([P, NP], F32, name="scaled")
+                scaled[step] = work.tile([P, NP], F32, name="scaled", bufs=4)
                 nc.vector.tensor_tensor(scaled[step][:], e_banks[step][:], row_sb[:], ALU.mult)
             if step > 0:
                 mt = step - 1
                 result = work.tile([P, NP], F32, name="result", bufs=4)
-                nc.vector.tensor_tensor(result[:], scaled[mt][:], order_sb[:, mt, :], ALU.add)
+                (nc.gpsimd if mt < 2 else nc.vector).tensor_tensor(result[:], scaled[mt][:], order_sb[:, mt, :], ALU.add)
                 nc.sync.dma_start(out=out[P * mt : P * (mt + 1), :], in_=result[:])

@@ -21,6 +21,7 @@ ACT = mybir.ActivationFunctionType
 P = 128
 BANK = 512
 TWO_PI = 2.0 * math.pi
+SUMMED = (2, 4, 6)
 
 
 def tile_list_bilingual_verse_correspondence_kernel(
@@ -36,7 +37,6 @@ def tile_list_bilingual_verse_correspondence_kernel(
         pos1_sb = keep.tile([P, NP // 16], U16, name="pos1_sb")
         pos2_sb = keep.tile([P, NP // 16], U16, name="pos2_sb")
         table = [keep.tile([P, T], I32, name="table%d" % a, tag="table%d" % a, align_bytes=64) for a in range(3)]
-        scales_raw = keep.tile([P, T], U8, name="scales_raw", align_bytes=64)
         table_scales = keep.tile([P, T], U8, name="table_scales", align_bytes=64)
         v_codes = [keep.tile([P, S], U32, name="v_codes%d" % a, align_bytes=64) for a in range(3)]
         v_scales = keep.tile([P, S], U8, name="v_scales", align_bytes=64)
@@ -49,11 +49,9 @@ def tile_list_bilingual_verse_correspondence_kernel(
         ident = keep.tile([P, P], F32, name="ident")
         factors = keep.tile([P, 2, 8], F32, name="factors")
         both = keep.tile([P, 2, 4], F32, name="both")
-        row_sb = keep.tile([P, NP], F32, name="row_sb")
-        order_sb = keep.tile([P, 4, NP], F32, name="order_sb")
 
         nc.vector.memset(table_scales[:].bitcast(I32), 0)
-        nc.vector.memset(w4s[:].bitcast(I32), 0)
+        nc.vector.memset(w4s_raw[:].bitcast(I32), 0)
         nc.vector.memset(v_scales1[:].bitcast(I32), 0)
         nc.gpsimd.memset(factors_raw[:], 0.0)
         for first, vec in ((0, gain), (4, latin)):
@@ -77,7 +75,7 @@ def tile_list_bilingual_verse_correspondence_kernel(
         load_table(0)
         for q in range(4):
             nc.sync.dma_start(
-                out=scales_raw[32 * q : 32 * q + 12, :].bitcast(I32),
+                out=table_scales[32 * q : 32 * q + 12, :].bitcast(I32),
                 in_=tab_scales[:, 4 * q : 4 * q + 4, :].bitcast(I32),
             )
         nc.sync.dma_start(
@@ -94,8 +92,6 @@ def tile_list_bilingual_verse_correspondence_kernel(
         load_table(1)
         nc.sync.dma_start(pos2_sb[:], pos2)
         nc.sync.dma_start(pos1_sb[:], pos1)
-        nc.sync.dma_start(out=order_sb[:], in_=order.rearrange("(mt p) j -> p mt j", p=P))
-        nc.sync.dma_start(out=row_sb[:], in_=row.partition_broadcast(P))
 
         turned = psum.tile([P, BANK], F32, name="bank")
         for b in range(2):
@@ -124,9 +120,6 @@ def tile_list_bilingual_verse_correspondence_kernel(
             w1_scales[i] = work.tile([P, P], U8, name="w1_scales", bufs=8, align_bytes=64)
             nc.vector.quantize_mx(out=w1_codes[i][:].bitcast(FP8X4), scales=w1_scales[i][:], in_=w1_bf[i][:])
 
-        for q in range(4):
-            rows = slice(32 * q, 32 * q + 12)
-            nc.vector.tensor_copy(table_scales[rows, :].bitcast(I32), scales_raw[rows, :].bitcast(I32))
         nc.vector.tensor_copy(v_scales[:], table_scales[:].indirect(offs_sb[:]))
         nc.scalar.dma_start(out=v_scales1[0:112, :].bitcast(I32), in_=v_scales[4:116, :].bitcast(I32))
         for half in range(2):
@@ -139,8 +132,7 @@ def tile_list_bilingual_verse_correspondence_kernel(
             )
 
         deal(w4_codes[:], w4_raw[:], 4)
-        for q in range(4):
-            deal(w4s[32 * q : 32 * q + 4, :], w4s_raw[32 * q : 32 * q + 4, :], 2)
+        deal(w4s[:], w4s_raw[:], 2)
         for i in range(4):
             round_w1(i)
             quantize_w1(i)
@@ -175,23 +167,39 @@ def tile_list_bilingual_verse_correspondence_kernel(
                 stop=(a == 1),
             )
 
+        positive = {}
         turns, angle, sine, read, picked, planes, x_codes, x_scales = {}, {}, {}, {}, {}, {}, {}, {}
 
         def count_turns(i):
-            g_sb = work.tile([P, S], F32, name="g_sb")
-            turns[i] = work.tile([P, S], I32, name="turns")
+            if i in SUMMED:
+                count = work.tile([P, S], U32, name="scratch")
+                turns[i] = keep.tile([P, S], F32, name="turns", tag="ring%d" % (i % 3))
+                positive[i] = work.tile([P, S], F32, name="positive")
+            else:
+                g_sb = work.tile([P, S], F32, name="scratch")
+                turns[i] = keep.tile([P, S], I32, name="turns", tag="ring%d" % (i % 3))
             for half in range(2):
                 cols = slice(BANK * half, BANK * (half + 1))
-                nc.scalar.copy(g_sb[:, cols], banks[i, half][:])
-                nc.gpsimd.tensor_scalar(turns[i][:, cols], g_sb[:, cols], 1.0 / TWO_PI, 0.0, ALU.mult, ALU.add)
+                if i in SUMMED:
+                    nc.scalar.activation(count[:, cols], banks[i, half][:], ACT.Relu, bias=0.0, scale=-1.0 / TWO_PI)
+                    nc.scalar.activation(turns[i][:, cols], count[:, cols], ACT.Copy, scale=TWO_PI)
+                    nc.scalar.activation(positive[i][:, cols], banks[i, half][:], ACT.Relu)
+                else:
+                    nc.scalar.copy(g_sb[:, cols], banks[i, half][:])
+                    nc.gpsimd.tensor_scalar(turns[i][:, cols], g_sb[:, cols], 1.0 / TWO_PI, 0.0, ALU.mult, ALU.add)
 
         def reduce_angle(i):
             angle[i] = work.tile([P, S], F32, name="angle", bufs=3)
             for half in range(2):
                 cols = slice(BANK * half, BANK * (half + 1))
-                nc.vector.scalar_tensor_tensor(
-                    angle[i][:, cols], turns[i][:, cols], -TWO_PI, banks[i, half][:], ALU.mult, ALU.add
-                )
+                if i in SUMMED:
+                    nc.vector.scalar_tensor_tensor(
+                        angle[i][:, cols], banks[i, half][:], 0.0, turns[i][:, cols], ALU.min, ALU.add
+                    )
+                else:
+                    nc.vector.scalar_tensor_tensor(
+                        angle[i][:, cols], turns[i][:, cols], -TWO_PI, banks[i, half][:], ALU.mult, ALU.add
+                    )
 
         def take_sine(i):
             sine[i] = work.tile([P, S], F32, name="sine")
@@ -203,22 +211,27 @@ def tile_list_bilingual_verse_correspondence_kernel(
             read[i] = work.tile([P, S], F32, name="read", bufs=3)
             for half in range(2):
                 cols = slice(BANK * half, BANK * (half + 1))
-                nc.vector.tensor_tensor(read[i][:, cols], banks[i, half][:], sine[i][:, cols], ALU.max)
+                if i in SUMMED:
+                    nc.gpsimd.tensor_tensor(read[i][:, cols], positive[i][:, cols], sine[i][:, cols], ALU.add)
+                else:
+                    nc.vector.tensor_tensor(read[i][:, cols], banks[i, half][:], sine[i][:, cols], ALU.max)
 
         def pick(i):
-            for side, pos in ((2, pos2_sb), (1, pos1_sb)):
-                picked[side, i] = work.tile([P, NP], F32, name="picked", bufs=4)
-                nc.vector.tensor_copy(picked[side, i][:], read[i][:].indirect(pos[:]))
+            tag = "ring%d" % ((i + 2) % 3) if i else "picked_first"
+            both_picks = keep.tile([P, 2, NP], F32, name="picked", tag=tag)
+            for slot, (side, pos) in enumerate(((2, pos2_sb), (1, pos1_sb))):
+                picked[side, i] = both_picks[:, slot, :]
+                nc.vector.tensor_copy(picked[side, i], read[i][:].indirect(pos[:]))
 
         def scale_and_round(i):
             b, t = divmod(i, 4)
-            for side, func, factor in (
-                (2, ACT.Abs, factors[:, b, t : t + 1]),
-                (1, ACT.Copy, both[:, b, t : t + 1]),
-            ):
-                if t == 0:
+            if t == 0:
+                for side in (2, 1):
                     planes[side, b] = work.tile([P, 4, NP], BF16, name="planes", bufs=4)
-                nc.scalar.activation(planes[side, b][:, t, :], picked[side, i][:], func, scale=factor)
+            nc.scalar.activation(planes[2, b][:, t, :], picked[2, i], ACT.Abs, scale=factors[:, b, t : t + 1])
+            nc.gpsimd.tensor_scalar(
+                planes[1, b][:, t, :], picked[1, i], both[:, b, t : t + 1], 0.0, ALU.mult, ALU.add
+            )
 
         def weave(copy, side, b, cols):
             copy(
@@ -265,26 +278,38 @@ def tile_list_bilingual_verse_correspondence_kernel(
 
         count_turns(0)
         reduce_angle(0)
+        take_sine(0)
+        take_max(0)
+        count_turns(1)
+        reduce_angle(1)
+        count_turns(2)
+        round_w1(4)
+        quantize_w1(4)
         for step in range(8):
-            if 4 <= step + 3 < 8:
+            if step + 4 < 8:
                 for half in range(2):
                     for a in (0, 2, 1):
-                        stage1_pass(step + 3, half, a)
-            take_sine(step)
-            take_max(step)
+                        stage1_pass(step + 4, half, a)
+            if step + 2 < 8:
+                reduce_angle(step + 2)
             pick(step)
-            for ahead in range(max(1, step + 2 if step else 1), min(step + 3, 8)):
-                count_turns(ahead)
-                reduce_angle(ahead)
-            if step < 4:
-                round_w1(step + 4)
-                quantize_w1(step + 4)
+            if step + 1 < 8:
+                take_sine(step + 1)
+                take_max(step + 1)
+            if step + 3 < 8:
+                count_turns(step + 3)
+            if step + 5 < 8:
+                round_w1(step + 5)
+                quantize_w1(step + 5)
             if step > 0:
                 scale_and_round(step - 1)
-            if step in (5, 6):
-                side = 7 - step
+            if step in (4, 5):
+                side = 6 - step
                 weave(nc.scalar.copy, side, 0, whole)
                 quantize_x(side, 0, whole)
+        last = keep.tile([P, 5, NP], F32, name="last", tag="table1", align_bytes=64)
+        nc.sync.dma_start(out=last[:, 0:4, :], in_=order.rearrange("(mt p) j -> p mt j", p=P))
+        nc.sync.dma_start(out=last[:, 4, :], in_=row.partition_broadcast(P))
         for mt in range(4):
             stage2_pass(mt, 0)
         scale_and_round(7)
@@ -299,9 +324,9 @@ def tile_list_bilingual_verse_correspondence_kernel(
         for step in range(5):
             if step < 4:
                 scaled[step] = work.tile([P, NP], F32, name="scaled", bufs=4)
-                nc.vector.tensor_tensor(scaled[step][:], e_banks[step][:], row_sb[:], ALU.mult)
+                nc.vector.tensor_tensor(scaled[step][:], e_banks[step][:], last[:, 4, :], ALU.mult)
             if step > 0:
                 mt = step - 1
                 result = work.tile([P, NP], F32, name="result", bufs=4)
-                (nc.gpsimd if mt < 2 else nc.vector).tensor_tensor(result[:], scaled[mt][:], order_sb[:, mt, :], ALU.add)
+                (nc.gpsimd if mt < 2 else nc.vector).tensor_tensor(result[:], scaled[mt][:], last[:, mt, :], ALU.add)
                 nc.sync.dma_start(out=out[P * mt : P * (mt + 1), :], in_=result[:])

@@ -41,28 +41,35 @@ def tile_list_bilingual_verse_correspondence_kernel(
         v_codes = [keep.tile([P, S], U32, name="v_codes%d" % a, align_bytes=64) for a in range(3)]
         v_scales = keep.tile([P, S], U8, name="v_scales", align_bytes=64)
         v_scales1 = keep.tile([P, S], U8, name="v_scales1", align_bytes=64)
-        w4_raw = keep.tile([P, 2 * 2 * H], U8, name="w4_raw", align_bytes=64)
-        w4_codes = keep.tile([P, 2 * 2 * H], U8, name="w4_codes", align_bytes=64)
+        w4_raw = [keep.tile([P, 2 * H], U8, name="w4_raw%d" % b, align_bytes=64) for b in range(2)]
+        w4_codes = [keep.tile([P, 2 * H], U8, name="w4_codes%d" % b, align_bytes=64) for b in range(2)]
         w4s_raw = keep.tile([P, 2 * H], U8, name="w4s_raw", align_bytes=64)
         w4s = keep.tile([P, 2 * H], U8, name="w4s", align_bytes=64)
-        factors_raw = keep.tile([P, 2 * P], F32, name="factors_raw")
+        factors_raw = keep.tile([4, BANK], F32, name="factors_raw")
+        factors_dealt = keep.tile([P, BANK], F32, name="factors_dealt")
         ident = keep.tile([P, P], F32, name="ident")
-        factors = keep.tile([P, 2, 8], F32, name="factors")
-        both = keep.tile([P, 2, 4], F32, name="both")
+        factors = keep.tile([P, 4, 4], F32, name="factors")
+        both = keep.tile([P, 4, 2], F32, name="both")
 
         nc.vector.memset(table_scales[:].bitcast(I32), 0)
-        nc.vector.memset(w4s_raw[:].bitcast(I32), 0)
-        nc.vector.memset(v_scales1[:].bitcast(I32), 0)
-        nc.gpsimd.memset(factors_raw[:], 0.0)
-        for first, vec in ((0, gain), (4, latin)):
+        nc.gpsimd.memset(w4s_raw[:].bitcast(I32), 0)
+        for q in range(4):
             nc.gpsimd.dma_start(
-                out=factors_raw[first : first + 4, :].rearrange("t (bq i) -> t bq i", i=8),
-                in_=vec.rearrange("(bq t i) -> t bq i", t=4, i=8),
+                out=table_scales[32 * q : 32 * q + 12, :].bitcast(I32),
+                in_=tab_scales[:, 4 * q : 4 * q + 4, :].bitcast(I32),
             )
+        nc.vector.memset(v_scales1[:].bitcast(I32), 0)
+        nc.vector.memset(factors_dealt[:], 0.0)
         make_identity(nc, ident[:])
 
         def load_table(a):
             nc.sync.dma_start(out=table[a][:], in_=tab_words[a].rearrange("p t i -> p (t i)").bitcast(I32))
+
+        def load_w4(b):
+            nc.sync.dma_start(
+                out=w4_raw[b][:].bitcast(I32).rearrange("p (a c) -> p a c", a=2),
+                in_=w4_words[:, :, H * b : H * (b + 1)].bitcast(I32).rearrange("a p c -> p a c"),
+            )
 
         w1_rows = w1.rearrange("(p j) c -> p j c", j=4)
         w1_raw = {}
@@ -75,29 +82,28 @@ def tile_list_bilingual_verse_correspondence_kernel(
         load_table(0)
         for q in range(4):
             nc.sync.dma_start(
-                out=table_scales[32 * q : 32 * q + 12, :].bitcast(I32),
-                in_=tab_scales[:, 4 * q : 4 * q + 4, :].bitcast(I32),
-            )
-        nc.sync.dma_start(
-            out=w4_raw[:].bitcast(I32).rearrange("p (a c) -> p a c", a=2),
-            in_=w4_words.bitcast(I32).rearrange("a p c -> p a c"),
-        )
-        load_w1(0, "w1_first")
-        for q in range(4):
-            nc.sync.dma_start(
                 out=w4s_raw[32 * q : 32 * q + 4, :].bitcast(I32).rearrange("r (a c) -> r a c", a=2),
                 in_=w4_scales[:, 4 * q : 4 * q + 4, :].bitcast(I32).rearrange("a r c -> r a c"),
             )
+        load_w4(0)
+        load_w1(0, "w1_first")
+        nc.sync.dma_start(out=factors_raw[0:2, :], in_=gain.rearrange("(b c) -> b c", b=2))
+        nc.sync.dma_start(out=factors_raw[2:4, :], in_=latin.rearrange("(b c) -> b c", b=2))
         load_table(2)
         load_table(1)
+        load_w4(1)
         nc.sync.dma_start(pos2_sb[:], pos2)
         nc.sync.dma_start(pos1_sb[:], pos1)
 
+        nc.scalar.copy(
+            out=factors_dealt[0:4, :].rearrange("r (t q i) -> r t q i", t=4, i=8),
+            in_=factors_raw[:].rearrange("r (q t i) -> r t q i", t=4, i=8),
+        )
         turned = psum.tile([P, BANK], F32, name="bank")
-        for b in range(2):
-            nc.tensor.transpose(turned[:, P * b : P * (b + 1)], factors_raw[:, P * b : P * (b + 1)], ident[:])
-        nc.scalar.copy(out=factors[:], in_=turned[:, 0 : 2 * P].rearrange("p (b c) -> p b c", b=2)[:, :, 0:8])
-        nc.gpsimd.tensor_tensor(both[:], factors[:, :, 0:4], factors[:, :, 4:8], ALU.mult)
+        for t in range(4):
+            nc.tensor.transpose(turned[:, P * t : P * (t + 1)], factors_dealt[:, P * t : P * (t + 1)], ident[:])
+        nc.scalar.copy(out=factors[:], in_=turned[:].rearrange("p (t c) -> p t c", t=4)[:, :, 0:4])
+        nc.gpsimd.tensor_tensor(both[:], factors[:, :, 0:2], factors[:, :, 2:4], ALU.mult)
 
         def gather_table(a, half):
             cols = slice(BANK * half, BANK * (half + 1))
@@ -131,7 +137,7 @@ def tile_list_bilingual_verse_correspondence_kernel(
                 in_=raw.bitcast(I32).rearrange("p (g q t w) -> p g t q w", t=4, q=16, w=w),
             )
 
-        deal(w4_codes[:], w4_raw[:], 4)
+        deal(w4_codes[0][:], w4_raw[0][:], 4)
         deal(w4s[:], w4s_raw[:], 2)
         for i in range(4):
             round_w1(i)
@@ -141,6 +147,7 @@ def tile_list_bilingual_verse_correspondence_kernel(
                 gather_table(a, half)
 
         load_w1(1, "table1")
+        deal(w4_codes[1][:], w4_raw[1][:], 4)
 
         banks = {}
 
@@ -150,7 +157,8 @@ def tile_list_bilingual_verse_correspondence_kernel(
                 banks[i, half] = psum.tile([P, BANK], F32, name="bank")
             if a < 2:
                 c0 = H * a + P * i
-                lhsT = w4_codes[:, 2 * c0 : 2 * (c0 + P)].bitcast(FP4X4)
+                c1 = BANK * a + P * (i % 4)
+                lhsT = w4_codes[i // 4][:, 2 * c1 : 2 * (c1 + P)].bitcast(FP4X4)
                 lhsT_scale = w4s[:, c0 : c0 + P]
                 rhs_scale = (v_scales, v_scales1)[a][:, cols]
             else:
@@ -228,9 +236,9 @@ def tile_list_bilingual_verse_correspondence_kernel(
             if t == 0:
                 for side in (2, 1):
                     planes[side, b] = work.tile([P, 4, NP], BF16, name="planes", bufs=4)
-            nc.scalar.activation(planes[2, b][:, t, :], picked[2, i], ACT.Abs, scale=factors[:, b, t : t + 1])
+            nc.scalar.activation(planes[2, b][:, t, :], picked[2, i], ACT.Abs, scale=factors[:, t, b : b + 1])
             nc.gpsimd.tensor_scalar(
-                planes[1, b][:, t, :], picked[1, i], both[:, b, t : t + 1], 0.0, ALU.mult, ALU.add
+                planes[1, b][:, t, :], picked[1, i], both[:, t, b : b + 1], 0.0, ALU.mult, ALU.add
             )
 
         def weave(copy, side, b, cols):

import math
from contextlib import ExitStack

import concourse.mybir as mybir
from concourse.masks import make_identity

K, KL, KM, H, T, S, NP = 1536, 1024, 512, 1024, 4096, 1024, 512
FLOPS = 2 * K * H * S + 2 * H * NP * NP

F32 = mybir.dt.float32
BF16 = mybir.dt.bfloat16
I32 = mybir.dt.int32
U32 = mybir.dt.uint32
U16 = mybir.dt.uint16
U8 = mybir.dt.uint8
FP8X4 = mybir.dt.float8_e4m3fn_x4
FP4X4 = mybir.dt.float4_e2m1fn_x4
ALU = mybir.AluOpType
ACT = mybir.ActivationFunctionType

P = 128
BANK = 512
TWO_PI = 2.0 * math.pi
SUMMED = (2, 4, 6)


def tile_list_bilingual_verse_correspondence_kernel(
    tc, tab_words, tab_scales, offs, pos1, pos2, w4_words, w4_scales, w1, gain, latin, row, order, out
):
    nc = tc.nc
    with ExitStack() as ctx:
        keep = ctx.enter_context(tc.tile_pool(name="keep", bufs=1))
        work = ctx.enter_context(tc.tile_pool(name="work", bufs=2))
        psum = ctx.enter_context(tc.psum_pool(name="psum", bufs=8))

        offs_sb = keep.tile([P, S // 16], U16, name="offs_sb")
        pos1_sb = keep.tile([P, NP // 16], U16, name="pos1_sb")
        pos2_sb = keep.tile([P, NP // 16], U16, name="pos2_sb")
        table = [keep.tile([P, T], I32, name="table%d" % a, tag="table%d" % a, align_bytes=64) for a in range(3)]
        table_scales = keep.tile([P, T], U8, name="table_scales", align_bytes=64)
        v_codes = [keep.tile([P, S], U32, name="v_codes%d" % a, align_bytes=64) for a in range(3)]
        v_scales = keep.tile([P, S], U8, name="v_scales", align_bytes=64)
        v_scales1 = keep.tile([P, S], U8, name="v_scales1", align_bytes=64)
        w4_raw = [keep.tile([P, 2 * H], U8, name="w4_raw%d" % b, align_bytes=64) for b in range(2)]
        w4_codes = [keep.tile([P, 2 * H], U8, name="w4_codes%d" % b, align_bytes=64) for b in range(2)]
        w4s_raw = keep.tile([P, 2 * H], U8, name="w4s_raw", align_bytes=64)
        w4s = keep.tile([P, 2 * H], U8, name="w4s", align_bytes=64)
        factors_raw = keep.tile([4, BANK], F32, name="factors_raw")
        factors_dealt = keep.tile([P, BANK], F32, name="factors_dealt")
        ident = keep.tile([P, P], F32, name="ident")
        factors = keep.tile([P, 4, 4], F32, name="factors")
        both = keep.tile([P, 4, 2], F32, name="both")

        nc.vector.memset(table_scales[:].bitcast(I32), 0)
        nc.gpsimd.memset(w4s_raw[:].bitcast(I32), 0)
        for q in range(4):
            nc.gpsimd.dma_start(
                out=table_scales[32 * q : 32 * q + 12, :].bitcast(I32),
                in_=tab_scales[:, 4 * q : 4 * q + 4, :].bitcast(I32),
            )
        nc.vector.memset(v_scales1[:].bitcast(I32), 0)
        nc.vector.memset(factors_dealt[:], 0.0)
        make_identity(nc, ident[:])

        def load_table(a):
            nc.sync.dma_start(out=table[a][:], in_=tab_words[a].rearrange("p t i -> p (t i)").bitcast(I32))

        def load_w4(b):
            nc.sync.dma_start(
                out=w4_raw[b][:].bitcast(I32).rearrange("p (a c) -> p a c", a=2),
                in_=w4_words[:, :, H * b : H * (b + 1)].bitcast(I32).rearrange("a p c -> p a c"),
            )

        w1_rows = w1.rearrange("(p j) c -> p j c", j=4)
        w1_raw = {}

        def load_w1(b, tag):
            w1_raw[b] = keep.tile([P, 4, BANK], F32, name="w1_raw%d" % b, tag=tag, align_bytes=64)
            nc.sync.dma_start(out=w1_raw[b][:], in_=w1_rows[:, :, BANK * b : BANK * (b + 1)])

        nc.sync.dma_start(offs_sb[:], offs)
        load_table(0)
        for q in range(4):
            nc.sync.dma_start(
                out=w4s_raw[32 * q : 32 * q + 4, :].bitcast(I32).rearrange("r (a c) -> r a c", a=2),
                in_=w4_scales[:, 4 * q : 4 * q + 4, :].bitcast(I32).rearrange("a r c -> r a c"),
            )
        load_w4(0)
        load_w1(0, "w1_first")
        nc.sync.dma_start(out=factors_raw[0:2, :], in_=gain.rearrange("(b c) -> b c", b=2))
        nc.sync.dma_start(out=factors_raw[2:4, :], in_=latin.rearrange("(b c) -> b c", b=2))
        load_table(2)
        load_table(1)
        load_w4(1)
        nc.sync.dma_start(pos2_sb[:], pos2)
        nc.sync.dma_start(pos1_sb[:], pos1)

        nc.scalar.copy(
            out=factors_dealt[0:4, :].rearrange("r (t q i) -> r t q i", t=4, i=8),
            in_=factors_raw[:].rearrange("r (q t i) -> r t q i", t=4, i=8),
        )
        turned = psum.tile([P, BANK], F32, name="bank")
        for t in range(4):
            nc.tensor.transpose(turned[:, P * t : P * (t + 1)], factors_dealt[:, P * t : P * (t + 1)], ident[:])
        nc.scalar.copy(out=factors[:], in_=turned[:].rearrange("p (t c) -> p t c", t=4)[:, :, 0:4])
        nc.gpsimd.tensor_tensor(both[:], factors[:, :, 0:2], factors[:, :, 2:4], ALU.mult)

        def gather_table(a, half):
            cols = slice(BANK * half, BANK * (half + 1))
            nc.vector.tensor_copy(
                v_codes[a][:, cols], table[a][:].bitcast(U32).indirect(offs_sb[:, 32 * half : 32 * (half + 1)])
            )

        w1_codes, w1_scales, w1_bf = {}, {}, {}

        def round_w1(i):
            b, t = divmod(i, 4)
            w1_bf[i] = work.tile([P, BANK], BF16, name="w1_bf", align_bytes=64)
            nc.scalar.copy(
                out=w1_bf[i][:].rearrange("p (q h l j) -> p q h j l", h=2, l=4, j=4),
                in_=w1_raw[b][:].rearrange("p j (q t h l) -> p t q h j l", t=4, h=2, l=4)[:, t],
            )

        def quantize_w1(i):
            w1_codes[i] = work.tile([P, P], U32, name="w1_codes", bufs=8, align_bytes=64)
            w1_scales[i] = work.tile([P, P], U8, name="w1_scales", bufs=8, align_bytes=64)
            nc.vector.quantize_mx(out=w1_codes[i][:].bitcast(FP8X4), scales=w1_scales[i][:], in_=w1_bf[i][:])

        nc.vector.tensor_copy(v_scales[:], table_scales[:].indirect(offs_sb[:]))
        nc.scalar.dma_start(out=v_scales1[0:112, :].bitcast(I32), in_=v_scales[4:116, :].bitcast(I32))
        for half in range(2):
            gather_table(0, half)

        def deal(dealt, raw, w):
            nc.vector.tensor_copy(
                out=dealt.bitcast(I32).rearrange("p (g t q w) -> p g t q w", t=4, q=16, w=w),
                in_=raw.bitcast(I32).rearrange("p (g q t w) -> p g t q w", t=4, q=16, w=w),
            )

        deal(w4_codes[0][:], w4_raw[0][:], 4)
        deal(w4s[:], w4s_raw[:], 2)
        for i in range(4):
            round_w1(i)
            quantize_w1(i)
        for a in (2, 1):
            for half in range(2):
                gather_table(a, half)

        load_w1(1, "table1")
        deal(w4_codes[1][:], w4_raw[1][:], 4)

        banks = {}

        def stage1_pass(i, half, a):
            cols = slice(BANK * half, BANK * (half + 1))
            if a == 0:
                banks[i, half] = psum.tile([P, BANK], F32, name="bank")
            if a < 2:
                c0 = H * a + P * i
                c1 = BANK * a + P * (i % 4)
                lhsT = w4_codes[i // 4][:, 2 * c1 : 2 * (c1 + P)].bitcast(FP4X4)
                lhsT_scale = w4s[:, c0 : c0 + P]
                rhs_scale = (v_scales, v_scales1)[a][:, cols]
            else:
                lhsT = w1_codes[i][:].bitcast(FP8X4)
                lhsT_scale = w1_scales[i][:]
                rhs_scale = v_scales[8:P, cols]
            nc.tensor.matmul_mx(
                out=banks[i, half][:],
                lhsT=lhsT,
                lhsT_scale=lhsT_scale,
                rhs=v_codes[a][:, cols].bitcast(FP8X4),
                rhs_scale=rhs_scale,
                start=(a == 0),
                stop=(a == 1),
            )

        positive = {}
        turns, angle, sine, read, picked, planes, x_codes, x_scales = {}, {}, {}, {}, {}, {}, {}, {}

        def count_turns(i):
            if i in SUMMED:
                count = work.tile([P, S], U32, name="scratch")
                turns[i] = keep.tile([P, S], F32, name="turns", tag="ring%d" % (i % 3))
                positive[i] = work.tile([P, S], F32, name="positive")
            else:
                g_sb = work.tile([P, S], F32, name="scratch")
                turns[i] = keep.tile([P, S], I32, name="turns", tag="ring%d" % (i % 3))
            for half in range(2):
                cols = slice(BANK * half, BANK * (half + 1))
                if i in SUMMED:
                    nc.scalar.activation(count[:, cols], banks[i, half][:], ACT.Relu, bias=0.0, scale=-1.0 / TWO_PI)
                    nc.scalar.activation(turns[i][:, cols], count[:, cols], ACT.Copy, scale=TWO_PI)
                    nc.scalar.activation(positive[i][:, cols], banks[i, half][:], ACT.Relu)
                else:
                    nc.scalar.copy(g_sb[:, cols], banks[i, half][:])
                    nc.gpsimd.tensor_scalar(turns[i][:, cols], g_sb[:, cols], 1.0 / TWO_PI, 0.0, ALU.mult, ALU.add)

        def reduce_angle(i):
            angle[i] = work.tile([P, S], F32, name="angle", bufs=3)
            for half in range(2):
                cols = slice(BANK * half, BANK * (half + 1))
                if i in SUMMED:
                    nc.vector.scalar_tensor_tensor(
                        angle[i][:, cols], banks[i, half][:], 0.0, turns[i][:, cols], ALU.min, ALU.add
                    )
                else:
                    nc.vector.scalar_tensor_tensor(
                        angle[i][:, cols], turns[i][:, cols], -TWO_PI, banks[i, half][:], ALU.mult, ALU.add
                    )

        def take_sine(i):
            sine[i] = work.tile([P, S], F32, name="sine")
            for half in range(2):
                cols = slice(BANK * half, BANK * (half + 1))
                nc.scalar.activation(sine[i][:, cols], angle[i][:, cols], ACT.Sin)

        def take_max(i):
            read[i] = work.tile([P, S], F32, name="read", bufs=3)
            for half in range(2):
                cols = slice(BANK * half, BANK * (half + 1))
                if i in SUMMED:
                    nc.gpsimd.tensor_tensor(read[i][:, cols], positive[i][:, cols], sine[i][:, cols], ALU.add)
                else:
                    nc.vector.tensor_tensor(read[i][:, cols], banks[i, half][:], sine[i][:, cols], ALU.max)

        def pick(i):
            tag = "ring%d" % ((i + 2) % 3) if i else "picked_first"
            both_picks = keep.tile([P, 2, NP], F32, name="picked", tag=tag)
            for slot, (side, pos) in enumerate(((2, pos2_sb), (1, pos1_sb))):
                picked[side, i] = both_picks[:, slot, :]
                nc.vector.tensor_copy(picked[side, i], read[i][:].indirect(pos[:]))

        def scale_and_round(i):
            b, t = divmod(i, 4)
            if t == 0:
                for side in (2, 1):
                    planes[side, b] = work.tile([P, 4, NP], BF16, name="planes", bufs=4)
            nc.scalar.activation(planes[2, b][:, t, :], picked[2, i], ACT.Abs, scale=factors[:, t, b : b + 1])
            nc.gpsimd.tensor_scalar(
                planes[1, b][:, t, :], picked[1, i], both[:, t, b : b + 1], 0.0, ALU.mult, ALU.add
            )

        def weave(copy, side, b, cols):
            copy(
                out=woven[side, b][:, cols, :].rearrange("p (c l) t -> p c t l", l=4),
                in_=planes[side, b][:, :, cols].rearrange("p t (c l) -> p c t l", l=4),
            )

        def quantize_x(side, b, cols):
            nc.vector.quantize_mx(
                out=x_codes[side, b][:, cols].bitcast(FP8X4),
                scales=x_scales[side, b][:, cols],
                in_=woven[side, b][:, cols, :].rearrange("p c t -> p (c t)"),
            )

        def stage2_pass(mt, b):
            cols = slice(P * mt, P * (mt + 1))
            if b == 0:
                e_banks[mt] = psum.tile([P, BANK], F32, name="bank")
            nc.tensor.matmul_mx(
                out=e_banks[mt][:],
                lhsT=x_codes[1, b][:, cols].bitcast(FP8X4),
                lhsT_scale=x_scales[1, b][:, cols],
                rhs=x_codes[2, b][:].bitcast(FP8X4),
                rhs_scale=x_scales[2, b][:],
                start=(b == 0),
                stop=(b == 1),
            )

        woven, e_banks = {}, {}
        for b in range(2):
            for side in (2, 1):
                woven[side, b] = keep.tile([P, NP, 4], BF16, name="woven%d%d" % (side, b), align_bytes=64)
                x_codes[side, b] = keep.tile([P, NP], U32, name="x_codes%d%d" % (side, b), align_bytes=64)
                x_scales[side, b] = keep.tile([P, NP], U8, name="x_scales%d%d" % (side, b), align_bytes=64)
        whole = slice(0, NP)

        for a in (0, 2):
            for half in range(2):
                for i in range(4):
                    stage1_pass(i, half, a)
        for i in range(4):
            for half in range(2):
                stage1_pass(i, half, 1)

        count_turns(0)
        reduce_angle(0)
        take_sine(0)
        take_max(0)
        count_turns(1)
        reduce_angle(1)
        count_turns(2)
        round_w1(4)
        quantize_w1(4)
        for step in range(8):
            if step + 4 < 8:
                for half in range(2):
                    for a in (0, 2, 1):
                        stage1_pass(step + 4, half, a)
            if step + 2 < 8:
                reduce_angle(step + 2)
            pick(step)
            if step + 1 < 8:
                take_sine(step + 1)
                take_max(step + 1)
            if step + 3 < 8:
                count_turns(step + 3)
            if step + 5 < 8:
                round_w1(step + 5)
                quantize_w1(step + 5)
            if step > 0:
                scale_and_round(step - 1)
            if step in (4, 5):
                side = 6 - step
                weave(nc.scalar.copy, side, 0, whole)
                quantize_x(side, 0, whole)
        last = keep.tile([P, 5, NP], F32, name="last", tag="table1", align_bytes=64)
        nc.sync.dma_start(out=last[:, 0:4, :], in_=order.rearrange("(mt p) j -> p mt j", p=P))
        nc.sync.dma_start(out=last[:, 4, :], in_=row.partition_broadcast(P))
        for mt in range(4):
            stage2_pass(mt, 0)
        scale_and_round(7)
        weave(nc.vector.tensor_copy, 2, 1, whole)
        for mt in range(4):
            weave(nc.scalar.copy, 1, 1, slice(P * mt, P * (mt + 1)))
        quantize_x(2, 1, whole)
        for mt in range(4):
            quantize_x(1, 1, slice(P * mt, P * (mt + 1)))
            stage2_pass(mt, 1)
        scaled = {}
        for step in range(5):
            if step < 4:
                scaled[step] = work.tile([P, NP], F32, name="scaled", bufs=4)
                nc.vector.tensor_tensor(scaled[step][:], e_banks[step][:], last[:, 4, :], ALU.mult)
            if step > 0:
                mt = step - 1
                result = work.tile([P, NP], F32, name="result", bufs=4)
                (nc.gpsimd if mt < 2 else nc.vector).tensor_tensor(result[:], scaled[mt][:], last[:, mt, :], ALU.add)
                nc.sync.dma_start(out=out[P * mt : P * (mt + 1), :], in_=result[:])
